import numpy as np
import ml_dtypes


def mxq(x, axis, fmt="e4m3"):
    dtype, down = {"e4m3": (ml_dtypes.float8_e4m3fn, 7), "e5m2": (ml_dtypes.float8_e5m2, 14)}[fmt]
    v = np.moveaxis(np.asarray(x, np.float32).astype(ml_dtypes.bfloat16).astype(np.float64), axis, -1)
    blocks = v.reshape(v.shape[:-1] + (-1, 32))
    amax = np.abs(blocks).max(-1, keepdims=True)
    byte = np.maximum(np.where(amax > 0, np.frexp(amax)[1] - 1 + 127, 0) - down, 1)
    scale = np.exp2(byte - 127.0)
    codes = (blocks / scale).astype(np.float32).astype(dtype).astype(np.float64)
    return np.moveaxis((codes * scale).reshape(v.shape), -1, axis)


WIDE = False


def mx_kscale(k):
    if not WIDE:
        return np.ones(k)
    levels = np.array([10, -10, 5, -5, 0])
    if k % 512:
        return np.exp2(np.random.permutation(np.resize(levels, k // 32))).repeat(32)
    a = np.empty((k // 512, 16))
    for p in range(k // 512):
        a[p, :8] = np.random.permutation(np.resize(levels, 8))
        for g in range(8):
            far = levels[np.abs(levels - a[p, g]) >= 10]
            a[p, g + 8] = far[np.random.randint(len(far))]
    return np.exp2(a.ravel()).repeat(32)


def f64(x):
    return np.asarray(x).astype(np.float64)


def striped(idx):
    return np.tile(np.asarray(idx).reshape(-1, 16).T, (8, 1)).astype(np.uint16)


def unstriped(offs):
    return offs[:16].T.reshape(-1).astype(np.int64)


E2M1 = np.array([0.0, 0.5, 1.0, 1.5, 2.0, 3.0, 4.0, 6.0, -0.0, -0.5, -1.0, -1.5, -2.0, -3.0, -4.0, -6.0])


def pack_weight(w, fmt):
    k, n = w.shape
    w = f64(np.asarray(w, np.float32).astype(ml_dtypes.bfloat16)).reshape(k // 32, 32, n)
    amax = np.abs(w).max(1)
    if fmt == "e4m3":
        byte = np.frexp(amax)[1] - 1 + 127 - 7
    else:
        mant, ex = np.frexp(amax / 6.0)
        byte = np.where(mant > 0.5, ex, ex - 1) + 127
    byte = np.clip(np.where(amax > 0, byte, 1), 1, 254)
    scaled = (w * np.exp2(127.0 - byte)[:, None, :]).reshape(k, n).astype(np.float32)
    by_word = np.ascontiguousarray(scaled.reshape(k // 512, 128, 4, n).transpose(0, 1, 3, 2))
    if fmt == "e4m3":
        words = by_word.astype(ml_dtypes.float8_e4m3fn).view(np.uint8)
    else:
        c = by_word.astype(ml_dtypes.float4_e2m1fn).view(np.uint8) & 0xF
        words = (c[..., 0::2] | (c[..., 1::2] << 4)).reshape(k // 512, 128, 2 * n)
    return np.ascontiguousarray(words), np.ascontiguousarray(byte.astype(np.uint8).reshape(k // 512, 16, n))


def unpack_weight(words, scales, fmt):
    g, _, n = scales.shape
    words = np.ascontiguousarray(words).reshape(g, 128, n, -1)
    if fmt == "e4m3":
        vals = words.view(ml_dtypes.float8_e4m3fn).astype(np.float64)
    else:
        nib = np.empty((g, 128, n, 4), np.uint8)
        nib[..., 0::2] = words & 0xF
        nib[..., 1::2] = words >> 4
        vals = E2M1[nib]
    vals = vals * np.repeat(np.exp2(scales.astype(np.float64) - 127.0), 8, axis=1)[..., None]
    return vals.transpose(0, 1, 3, 2).reshape(g * 512, n)


D, K, T, U, I, E = 512, 512, 2048, 1024, 512, 256


def setup_inputs():
    n = np.random.standard_normal
    idx = np.random.permutation(T)[:I]
    idx2 = np.random.permutation(U)[:I]
    fd = mx_kscale(D)
    fk = mx_kscale(K)
    pagesp = pack_weight(n((D, T)) / fd[:, None], "e4m3")
    wap = pack_weight(n((D, K)) * 1.0 / np.sqrt(D) * fd[:, None], "e2m1")
    notesp = pack_weight(n((D, U)) / fd[:, None], "e2m1")
    wbp = pack_weight(n((D, K)) * 1.0 / np.sqrt(D) * fd[:, None], "e4m3")
    wop = pack_weight(n((K, E)) * 1.0 / np.sqrt(K) / fk[:, None], "e2m1")
    wpp = pack_weight(n((K, E)) * 1.0 / np.sqrt(K) / fk[:, None], "e4m3")
    return {
        "pages_words": pagesp[0],
        "pages_scales": pagesp[1],
        "wa_words": wap[0],
        "wa_scales": wap[1],
        "notes_words": notesp[0],
        "notes_scales": notesp[1],
        "wb_words": wbp[0],
        "wb_scales": wbp[1],
        "kf": (np.random.uniform(0.5, 2.0, (K, 1)) * fk[:, None]).astype(np.float32),
        "kf2": (np.random.uniform(0.5, 2.0, (K, 1)) * fk[:, None]).astype(np.float32),
        "wo_words": wop[0],
        "wo_scales": wop[1],
        "wp_words": wpp[0],
        "wp_scales": wpp[1],
        "offs": striped(idx),
        "offs2": striped(idx2),
    }


def reference(pages_words, pages_scales, wa_words, wa_scales, notes_words, notes_scales, wb_words, wb_scales, kf, kf2, wo_words, wo_scales, wp_words, wp_scales, offs, offs2):
    idx = unstriped(offs)
    idx2 = unstriped(offs2)
    pagesu = unpack_weight(pages_words, pages_scales, "e4m3")
    wau = unpack_weight(wa_words, wa_scales, "e2m1")
    notesu = unpack_weight(notes_words, notes_scales, "e2m1")
    wbu = unpack_weight(wb_words, wb_scales, "e4m3")
    wou = unpack_weight(wo_words, wo_scales, "e2m1")
    wpu = unpack_weight(wp_words, wp_scales, "e4m3")
    pagesidxg = pagesu[:, idx]
    z = wau.T @ pagesidxg
    h1 = wbu.T @ notesu
    w = z * f64(kf)
    w2 = h1[:, idx2] * f64(kf2)
    wq = mxq(w, 0, "e4m3")
    w2q = mxq(w2, 0, "e4m3")
    y = wou.T @ wq + wpu.T @ w2q
    return y

@@ -1,0 +1,197 @@
+from contextlib import ExitStack
+
+import concourse.mybir as mybir
+
+D, K, T, U, SLOTS, E = 512, 512, 2048, 1024, 512, 256
+FLOPS = 2 * D * K * SLOTS + 2 * D * K * U + 2 * 2 * K * E * SLOTS
+
+F32 = mybir.dt.float32
+BF16 = mybir.dt.bfloat16
+I32 = mybir.dt.int32
+U32 = mybir.dt.uint32
+U16 = mybir.dt.uint16
+U8 = mybir.dt.uint8
+FP8X4 = mybir.dt.float8_e4m3fn_x4
+FP4X4 = mybir.dt.float4_e2m1fn_x4
+MULT = mybir.AluOpType.mult
+COPY = mybir.ActivationFunctionType.Copy
+
+P = 128
+PACK = 4
+BANK = 512
+HALF = SLOTS // 2
+CHUNK = BANK // PACK
+
+
+def deal(nc, dst, src, run):
+    nc.vector.tensor_copy(
+        out=dst.rearrange("p (t c i) -> p c t i", t=PACK, i=run),
+        in_=src.rearrange("p (c i t) -> p c t i", t=PACK, i=run),
+    )
+
+
+def tile_attend_pagesandhidden_kernel(
+    tc, pages_words, pages_scales, wa_words, wa_scales, notes_words, notes_scales, wb_words, wb_scales,
+    kf, kf2, wo_words, wo_scales, wp_words, wp_scales, offs, offs2, out,
+):
+    nc = tc.nc
+    with ExitStack() as ctx:
+        keep = ctx.enter_context(tc.tile_pool(name="keep", bufs=1))
+        psum = ctx.enter_context(tc.psum_pool(name="psum", bufs=4))
+
+        def plane(name, width):
+            tile = keep.tile([P, width], U8, name=name, align_bytes=64)
+            nc.vector.memset(tile[:].bitcast(I32), 0)
+            return tile
+
+        def load_scale_rows(queue, tile, scales, quadrant):
+            queue.dma_start(
+                out=tile[:].bitcast(I32)[32 * quadrant : 32 * quadrant + 4, :],
+                in_=scales[0].bitcast(I32)[4 * quadrant : 4 * quadrant + 4, :],
+            )
+
+        def load_fp8(queue, name, words, width):
+            tile = keep.tile([P, width], I32, name=name, align_bytes=64)
+            queue.dma_start(out=tile[:], in_=words[0].rearrange("p n t -> p (n t)").bitcast(I32))
+            return tile
+
+        def load_fp4(queue, name, words, width):
+            tile = keep.tile([P, 2 * width], U8, name=name, align_bytes=64)
+            queue.dma_start(out=tile[:].bitcast(I32), in_=words[0].bitcast(I32))
+            return tile
+
+        wb_s = plane("wb_s", K)
+        notes_s = plane("notes_s", U)
+        pages_s = plane("pages_s", T)
+        wa_s = plane("wa_s", K)
+        wo_s = plane("wo_s", E)
+        wp_s = plane("wp_s", E)
+
+        both = (nc.sync, nc.scalar)
+        wb_w = load_fp8(nc.sync, "wb_w", wb_words, K)
+        notes_w = load_fp4(nc.scalar, "notes_w", notes_words, U)
+        for q in range(4):
+            load_scale_rows(both[q % 2], wb_s, wb_scales, q)
+        for q in range(4):
+            load_scale_rows(both[q % 2], notes_s, notes_scales, q)
+        for q in range(4):
+            load_scale_rows(both[q % 2], pages_s, pages_scales, q)
+        offsets = keep.tile([P, SLOTS // 16], U16, name="offsets")
+        nc.sync.dma_start(offsets[:], offs)
+        pages_w = load_fp8(nc.sync, "pages_w", pages_words, T)
+        wa_w = load_fp4(nc.sync, "wa_w", wa_words, K)
+        for q in range(4):
+            load_scale_rows(nc.sync, wa_s, wa_scales, q)
+        offsets2 = keep.tile([P, SLOTS // 16], U16, name="offsets2")
+        nc.sync.dma_start(offsets2[:], offs2)
+        kf_t = keep.tile([P, PACK], F32, name="kf_t")
+        nc.sync.dma_start(out=kf_t[:], in_=kf.rearrange("(p t) o -> p (t o)", t=PACK))
+        kf2_t = keep.tile([P, PACK], F32, name="kf2_t")
+        nc.sync.dma_start(out=kf2_t[:], in_=kf2.rearrange("(p t) o -> p (t o)", t=PACK))
+        wo_w = load_fp4(nc.sync, "wo_w", wo_words, E)
+        for q in range(4):
+            load_scale_rows(nc.sync, wo_s, wo_scales, q)
+        wp_w = load_fp8(nc.sync, "wp_w", wp_words, E)
+        for q in range(4):
+            load_scale_rows(nc.sync, wp_s, wp_scales, q)
+
+        wb_wd = keep.tile([P, K], U32, name="wb_wd", align_bytes=64)
+        deal(nc, wb_wd[:], wb_w[:].bitcast(U32), 4)
+        wb_sd = keep.tile([P, K], U8, name="wb_sd", align_bytes=64)
+        deal(nc, wb_sd[:], wb_s[:], 16)
+
+        h1 = [keep.tile([P, U], F32, name="h1_%d" % t) for t in range(PACK)]
+        for t in range(PACK):
+            for b in range(U // BANK):
+                acc = psum.tile([P, BANK], F32, name="acc")
+                nc.tensor.matmul_mx(
+                    out=acc[:],
+                    lhsT=wb_wd[:, t * P : (t + 1) * P].bitcast(FP8X4),
+                    lhsT_scale=wb_sd[:, t * P : (t + 1) * P],
+                    rhs=notes_w[:, 2 * b * BANK : 2 * (b + 1) * BANK].bitcast(FP4X4),
+                    rhs_scale=notes_s[:, b * BANK : (b + 1) * BANK],
+                    start=True,
+                    stop=True,
+                )
+                if t == 0 and b == 1:
+                    nc.vector.tensor_copy(out=h1[t][:, b * BANK : (b + 1) * BANK], in_=acc[:])
+                else:
+                    nc.scalar.copy(out=h1[t][:, b * BANK : (b + 1) * BANK], in_=acc[:])
+
+        picked_w = keep.tile([P, SLOTS], U32, name="picked_w", align_bytes=64)
+        nc.vector.tensor_copy(picked_w[:], pages_w[:].bitcast(U32).indirect(offsets[:]))
+        picked_s = keep.tile([P, SLOTS], U8, name="picked_s", align_bytes=64)
+        nc.vector.tensor_copy(picked_s[:], pages_s[:].indirect(offsets[:]))
+
+        wa_wd = keep.tile([P, 2 * K], U8, name="wa_wd", align_bytes=64)
+        deal(nc, wa_wd[:].bitcast(U16), wa_w[:].bitcast(U16), 8)
+        wa_sd = keep.tile([P, K], U8, name="wa_sd", align_bytes=64)
+        deal(nc, wa_sd[:], wa_s[:], 16)
+
+        w_bf = [keep.tile([P, HALF * PACK], BF16, name="w_bf%d" % h, align_bytes=64) for h in range(2)]
+        w_q = [keep.tile([P, HALF], U32, name="w_q%d" % h, align_bytes=64) for h in range(2)]
+        w_s = [keep.tile([P, HALF], U8, name="w_s%d" % h, align_bytes=64) for h in range(2)]
+        for h in range(2):
+            for c in range(HALF // CHUNK):
+                cols = slice(h * HALF + c * CHUNK, h * HALF + (c + 1) * CHUNK)
+                z = psum.tile([P, PACK, CHUNK], F32, name="z")
+                for t in range(PACK):
+                    nc.tensor.matmul_mx(
+                        out=z[:, t, :],
+                        lhsT=wa_wd[:, 2 * t * P : 2 * (t + 1) * P].bitcast(FP4X4),
+                        lhsT_scale=wa_sd[:, t * P : (t + 1) * P],
+                        rhs=picked_w[:, cols].bitcast(FP8X4),
+                        rhs_scale=picked_s[:, cols],
+                        start=True,
+                        stop=True,
+                    )
+                nc.vector.tensor_tensor(
+                    out=w_bf[h][:, c * BANK : (c + 1) * BANK].rearrange("p (i t) -> p i t", t=PACK),
+                    in0=z[:].rearrange("p t i -> p i t"),
+                    in1=kf_t[:].unsqueeze(1).to_broadcast([P, CHUNK, PACK]),
+                    op=MULT,
+                )
+        for h in range(2):
+            nc.vector.quantize_mx(out=w_q[h][:].bitcast(FP8X4), scales=w_s[h][:], in_=w_bf[h][:])
+
+        for h in range(2):
+            lists = offsets2[:, h * (HALF // 16) : (h + 1) * (HALF // 16)]
+            planes = keep.tile([P, PACK, HALF], BF16, name="planes%d" % h)
+            for t in range(PACK):
+                looked = keep.tile([P, HALF], F32, name="looked%d_%d" % (h, t))
+                nc.scalar.activation(looked[:], h1[t][:].indirect(lists), COPY)
+                nc.vector.tensor_scalar(planes[:, t, :], looked[:], kf2_t[:, t : t + 1], None, MULT)
+            w2_bf = keep.tile([P, HALF * PACK], BF16, name="w2_bf%d" % h, align_bytes=64)
+            nc.vector.tensor_copy(
+                out=w2_bf[:].rearrange("p (c i t) -> p c t i", t=PACK, i=4),
+                in_=planes[:].rearrange("p t (c i) -> p c t i", i=4),
+            )
+            w2_q = keep.tile([P, HALF], U32, name="w2_q%d" % h, align_bytes=64)
+            w2_s = keep.tile([P, HALF], U8, name="w2_s%d" % h, align_bytes=64)
+            nc.vector.quantize_mx(out=w2_q[:].bitcast(FP8X4), scales=w2_s[:], in_=w2_bf[:])
+            for a in range(E // P):
+                acc = psum.tile([P, HALF], F32, name="acc")
+                nc.tensor.matmul_mx(
+                    out=acc[:],
+                    lhsT=wo_w[:, 2 * a * P : 2 * (a + 1) * P].bitcast(FP4X4),
+                    lhsT_scale=wo_s[:, a * P : (a + 1) * P],
+                    rhs=w_q[h][:].bitcast(FP8X4),
+                    rhs_scale=w_s[h][:],
+                    start=True,
+                    stop=False,
+                )
+                nc.tensor.matmul_mx(
+                    out=acc[:],
+                    lhsT=wp_w[:, a * P : (a + 1) * P].bitcast(FP8X4),
+                    lhsT_scale=wp_s[:, a * P : (a + 1) * P],
+                    rhs=w2_q[:].bitcast(FP8X4),
+                    rhs_scale=w2_s[:],
+                    start=False,
+                    stop=True,
+                )
+                y = keep.tile([P, HALF], F32, name="y%d_%d" % (h, a))
+                if a == 0:
+                    nc.scalar.copy(out=y[:], in_=acc[:])
+                else:
+                    nc.vector.tensor_copy(out=y[:], in_=acc[:])
+                nc.sync.dma_start(out=out[a * P : (a + 1) * P, h * HALF : (h + 1) * HALF], in_=y[:])

@@ -21,6 +21,7 @@ PACK = 4
 BANK = 512
 HALF = SLOTS // 2
 CHUNK = BANK // PACK
+STRETCHES = (256, 128, 128)
 
 
 def deal(nc, dst, src, run):
@@ -39,9 +40,9 @@ def tile_attend_pagesandhidden_kernel(
         keep = ctx.enter_context(tc.tile_pool(name="keep", bufs=1))
         psum = ctx.enter_context(tc.psum_pool(name="psum", bufs=4))
 
-        def plane(name, width):
+        def plane(name, width, engine=nc.vector):
             tile = keep.tile([P, width], U8, name=name, align_bytes=64)
-            nc.vector.memset(tile[:].bitcast(I32), 0)
+            engine.memset(tile[:].bitcast(I32), 0)
             return tile
 
         def load_scale_rows(queue, tile, scales, quadrant):
@@ -62,30 +63,30 @@ def tile_attend_pagesandhidden_kernel(
 
         wb_s = plane("wb_s", K)
         notes_s = plane("notes_s", U)
-        pages_s = plane("pages_s", T)
+        pages_s = plane("pages_s", T, nc.gpsimd)
         wa_s = plane("wa_s", K)
         wo_s = plane("wo_s", E)
         wp_s = plane("wp_s", E)
 
-        both = (nc.sync, nc.scalar)
         wb_w = load_fp8(nc.sync, "wb_w", wb_words, K)
         notes_w = load_fp4(nc.scalar, "notes_w", notes_words, U)
         for q in range(4):
-            load_scale_rows(both[q % 2], wb_s, wb_scales, q)
-        for q in range(4):
-            load_scale_rows(both[q % 2], notes_s, notes_scales, q)
-        for q in range(4):
-            load_scale_rows(both[q % 2], pages_s, pages_scales, q)
+            load_scale_rows(nc.scalar if q else nc.sync, wb_s, wb_scales, q)
+        load_scale_rows(nc.sync, notes_s, notes_scales, 0)
+        pages_w = load_fp8(nc.sync, "pages_w", pages_words, T)
+        for q in range(1, 4):
+            load_scale_rows(nc.sync, notes_s, notes_scales, q)
         offsets = keep.tile([P, SLOTS // 16], U16, name="offsets")
         nc.sync.dma_start(offsets[:], offs)
-        pages_w = load_fp8(nc.sync, "pages_w", pages_words, T)
+        for q in range(4):
+            load_scale_rows(nc.gpsimd if q < 2 else nc.sync, pages_s, pages_scales, q)
         wa_w = load_fp4(nc.sync, "wa_w", wa_words, K)
+        kf_t = keep.tile([P, PACK], F32, name="kf_t")
+        nc.sync.dma_start(out=kf_t[:], in_=kf.rearrange("(p t) o -> p (t o)", t=PACK))
         for q in range(4):
             load_scale_rows(nc.sync, wa_s, wa_scales, q)
         offsets2 = keep.tile([P, SLOTS // 16], U16, name="offsets2")
         nc.sync.dma_start(offsets2[:], offs2)
-        kf_t = keep.tile([P, PACK], F32, name="kf_t")
-        nc.sync.dma_start(out=kf_t[:], in_=kf.rearrange("(p t) o -> p (t o)", t=PACK))
         kf2_t = keep.tile([P, PACK], F32, name="kf2_t")
         nc.sync.dma_start(out=kf2_t[:], in_=kf2.rearrange("(p t) o -> p (t o)", t=PACK))
         wo_w = load_fp4(nc.sync, "wo_w", wo_words, E)
@@ -100,6 +101,7 @@ def tile_attend_pagesandhidden_kernel(
         wb_sd = keep.tile([P, K], U8, name="wb_sd", align_bytes=64)
         deal(nc, wb_sd[:], wb_s[:], 16)
 
+
         h1 = [keep.tile([P, U], F32, name="h1_%d" % t) for t in range(PACK)]
         for t in range(PACK):
             for b in range(U // BANK):
@@ -113,15 +115,13 @@ def tile_attend_pagesandhidden_kernel(
                     start=True,
                     stop=True,
                 )
-                if t == 0 and b == 1:
-                    nc.vector.tensor_copy(out=h1[t][:, b * BANK : (b + 1) * BANK], in_=acc[:])
-                else:
-                    nc.scalar.copy(out=h1[t][:, b * BANK : (b + 1) * BANK], in_=acc[:])
+                nc.scalar.copy(out=h1[t][:, b * BANK : (b + 1) * BANK], in_=acc[:])
 
         picked_w = keep.tile([P, SLOTS], U32, name="picked_w", align_bytes=64)
         nc.vector.tensor_copy(picked_w[:], pages_w[:].bitcast(U32).indirect(offsets[:]))
         picked_s = keep.tile([P, SLOTS], U8, name="picked_s", align_bytes=64)
         nc.vector.tensor_copy(picked_s[:], pages_s[:].indirect(offsets[:]))
+
 
         wa_wd = keep.tile([P, 2 * K], U8, name="wa_wd", align_bytes=64)
         deal(nc, wa_wd[:].bitcast(U16), wa_w[:].bitcast(U16), 8)
@@ -129,8 +129,8 @@ def tile_attend_pagesandhidden_kernel(
         deal(nc, wa_sd[:], wa_s[:], 16)
 
         w_bf = [keep.tile([P, HALF * PACK], BF16, name="w_bf%d" % h, align_bytes=64) for h in range(2)]
-        w_q = [keep.tile([P, HALF], U32, name="w_q%d" % h, align_bytes=64) for h in range(2)]
-        w_s = [keep.tile([P, HALF], U8, name="w_s%d" % h, align_bytes=64) for h in range(2)]
+        w_q = keep.tile([P, SLOTS], U32, name="w_q", align_bytes=64)
+        w_s = keep.tile([P, SLOTS], U8, name="w_s", align_bytes=64)
         for h in range(2):
             for c in range(HALF // CHUNK):
                 cols = slice(h * HALF + c * CHUNK, h * HALF + (c + 1) * CHUNK)
@@ -152,46 +152,51 @@ def tile_attend_pagesandhidden_kernel(
                     op=MULT,
                 )
         for h in range(2):
-            nc.vector.quantize_mx(out=w_q[h][:].bitcast(FP8X4), scales=w_s[h][:], in_=w_bf[h][:])
+            cols = slice(h * HALF, (h + 1) * HALF)
+            nc.vector.quantize_mx(out=w_q[:, cols].bitcast(FP8X4), scales=w_s[:, cols], in_=w_bf[h][:])
 
-        for h in range(2):
-            lists = offsets2[:, h * (HALF // 16) : (h + 1) * (HALF // 16)]
-            planes = keep.tile([P, PACK, HALF], BF16, name="planes%d" % h)
+        first = 0
+        for h, n in enumerate(STRETCHES):
+            cols = slice(first, first + n)
+            lists = offsets2[:, first // 16 : (first + n) // 16]
+            first = first + n
+            looked = keep.tile([P, PACK, n], F32, name="looked%d" % h)
             for t in range(PACK):
-                looked = keep.tile([P, HALF], F32, name="looked%d_%d" % (h, t))
-                nc.scalar.activation(looked[:], h1[t][:].indirect(lists), COPY)
-                nc.vector.tensor_scalar(planes[:, t, :], looked[:], kf2_t[:, t : t + 1], None, MULT)
-            w2_bf = keep.tile([P, HALF * PACK], BF16, name="w2_bf%d" % h, align_bytes=64)
-            nc.vector.tensor_copy(
+                if h == 1 and t < 2:
+                    nc.vector.tensor_copy(looked[:, t, :], h1[t][:].indirect(lists))
+                else:
+                    nc.scalar.activation(looked[:, t, :], h1[t][:].indirect(lists), COPY)
+            w2_bf = keep.tile([P, n * PACK], BF16, name="w2_bf%d" % h, align_bytes=64)
+            nc.vector.tensor_tensor(
                 out=w2_bf[:].rearrange("p (c i t) -> p c t i", t=PACK, i=4),
-                in_=planes[:].rearrange("p t (c i) -> p c t i", i=4),
+                in0=looked[:].rearrange("p t (c i) -> p c t i", i=4),
+                in1=kf2_t[:].unsqueeze(1).unsqueeze(3).to_broadcast([P, n // 4, PACK, 4]),
+                op=MULT,
             )
-            w2_q = keep.tile([P, HALF], U32, name="w2_q%d" % h, align_bytes=64)
-            w2_s = keep.tile([P, HALF], U8, name="w2_s%d" % h, align_bytes=64)
+            w2_q = keep.tile([P, n], U32, name="w2_q%d" % h, align_bytes=64)
+            w2_s = keep.tile([P, n], U8, name="w2_s%d" % h, align_bytes=64)
             nc.vector.quantize_mx(out=w2_q[:].bitcast(FP8X4), scales=w2_s[:], in_=w2_bf[:])
+            acc = psum.tile([P, E // P, n], F32, name="acc")
             for a in range(E // P):
-                acc = psum.tile([P, HALF], F32, name="acc")
                 nc.tensor.matmul_mx(
-                    out=acc[:],
+                    out=acc[:, a, :],
                     lhsT=wo_w[:, 2 * a * P : 2 * (a + 1) * P].bitcast(FP4X4),
                     lhsT_scale=wo_s[:, a * P : (a + 1) * P],
-                    rhs=w_q[h][:].bitcast(FP8X4),
-                    rhs_scale=w_s[h][:],
-                    start=True,
+                    rhs=w_q[:, cols].bitcast(FP8X4),
+                    rhs_scale=w_s[:, cols],
+                    start=(a == 0),
                     stop=False,
                 )
+            for a in range(E // P):
                 nc.tensor.matmul_mx(
-                    out=acc[:],
+                    out=acc[:, a, :],
                     lhsT=wp_w[:, a * P : (a + 1) * P].bitcast(FP8X4),
                     lhsT_scale=wp_s[:, a * P : (a + 1) * P],
                     rhs=w2_q[:].bitcast(FP8X4),
                     rhs_scale=w2_s[:],
                     start=False,
-                    stop=True,
+                    stop=(a == E // P - 1),
                 )
-                y = keep.tile([P, HALF], F32, name="y%d_%d" % (h, a))
-                if a == 0:
-                    nc.scalar.copy(out=y[:], in_=acc[:])
-                else:
-                    nc.vector.tensor_copy(out=y[:], in_=acc[:])
-                nc.sync.dma_start(out=out[a * P : (a + 1) * P, h * HALF : (h + 1) * HALF], in_=y[:])
+            y = keep.tile([P, E // P, n], F32, name="y%d" % h)
+            nc.scalar.copy(out=y[:], in_=acc[:])
+            nc.sync.dma_start(out=out[:, cols].rearrange("(a p) i -> p a i", p=P), in_=y[:])

@@ -38,7 +38,7 @@ def tile_attend_pagesandhidden_kernel(
     nc = tc.nc
     with ExitStack() as ctx:
         keep = ctx.enter_context(tc.tile_pool(name="keep", bufs=1))
-        psum = ctx.enter_context(tc.psum_pool(name="psum", bufs=4))
+        psum = ctx.enter_context(tc.psum_pool(name="psum", bufs=8))
 
         def plane(name, width, engine=nc.vector):
             tile = keep.tile([P, width], U8, name=name, align_bytes=64)
@@ -117,31 +117,32 @@ def tile_attend_pagesandhidden_kernel(
                 )
                 nc.scalar.copy(out=h1[t][:, b * BANK : (b + 1) * BANK], in_=acc[:])
 
-        picked_w = keep.tile([P, SLOTS], U32, name="picked_w", align_bytes=64)
-        nc.vector.tensor_copy(picked_w[:], pages_w[:].bitcast(U32).indirect(offsets[:]))
-        picked_s = keep.tile([P, SLOTS], U8, name="picked_s", align_bytes=64)
-        nc.vector.tensor_copy(picked_s[:], pages_s[:].indirect(offsets[:]))
-
-
+        picked_w = [keep.tile([P, HALF], U32, name="picked_w%d" % h, align_bytes=64) for h in range(2)]
+        picked_s = [keep.tile([P, HALF], U8, name="picked_s%d" % h, align_bytes=64) for h in range(2)]
+        halves = [offsets[:, h * (HALF // 16) : (h + 1) * (HALF // 16)] for h in range(2)]
+        nc.vector.tensor_copy(picked_w[0][:], pages_w[:].bitcast(U32).indirect(halves[0]))
+        nc.vector.tensor_copy(picked_s[0][:], pages_s[:].indirect(halves[0]))
+        nc.vector.tensor_copy(picked_w[1][:], pages_w[:].bitcast(U32).indirect(halves[1]))
         wa_wd = keep.tile([P, 2 * K], U8, name="wa_wd", align_bytes=64)
         deal(nc, wa_wd[:].bitcast(U16), wa_w[:].bitcast(U16), 8)
         wa_sd = keep.tile([P, K], U8, name="wa_sd", align_bytes=64)
         deal(nc, wa_sd[:], wa_s[:], 16)
+        nc.vector.tensor_copy(picked_s[1][:], pages_s[:].indirect(halves[1]))
 
         w_bf = [keep.tile([P, HALF * PACK], BF16, name="w_bf%d" % h, align_bytes=64) for h in range(2)]
         w_q = keep.tile([P, SLOTS], U32, name="w_q", align_bytes=64)
         w_s = keep.tile([P, SLOTS], U8, name="w_s", align_bytes=64)
         for h in range(2):
             for c in range(HALF // CHUNK):
-                cols = slice(h * HALF + c * CHUNK, h * HALF + (c + 1) * CHUNK)
-                z = psum.tile([P, PACK, CHUNK], F32, name="z")
+                cols = slice(c * CHUNK, (c + 1) * CHUNK)
+                z = psum.tile([P, PACK, CHUNK], F32, name="acc")
                 for t in range(PACK):
                     nc.tensor.matmul_mx(
                         out=z[:, t, :],
                         lhsT=wa_wd[:, 2 * t * P : 2 * (t + 1) * P].bitcast(FP4X4),
                         lhsT_scale=wa_sd[:, t * P : (t + 1) * P],
-                        rhs=picked_w[:, cols].bitcast(FP8X4),
-                        rhs_scale=picked_s[:, cols],
+                        rhs=picked_w[h][:, cols].bitcast(FP8X4),
+                        rhs_scale=picked_s[h][:, cols],
                         start=True,
                         stop=True,
                     )

from contextlib import ExitStack

import concourse.mybir as mybir

D, K, T, U, SLOTS, E = 512, 512, 2048, 1024, 512, 256
FLOPS = 2 * D * K * SLOTS + 2 * D * K * U + 2 * 2 * K * E * SLOTS

F32 = mybir.dt.float32
BF16 = mybir.dt.bfloat16
I32 = mybir.dt.int32
U32 = mybir.dt.uint32
U16 = mybir.dt.uint16
U8 = mybir.dt.uint8
FP8X4 = mybir.dt.float8_e4m3fn_x4
FP4X4 = mybir.dt.float4_e2m1fn_x4
MULT = mybir.AluOpType.mult
COPY = mybir.ActivationFunctionType.Copy

P = 128
PACK = 4
BANK = 512
HALF = SLOTS // 2
CHUNK = BANK // PACK
STRETCHES = (256, 128, 128)


def deal(nc, dst, src, run):
    nc.vector.tensor_copy(
        out=dst.rearrange("p (t c i) -> p c t i", t=PACK, i=run),
        in_=src.rearrange("p (c i t) -> p c t i", t=PACK, i=run),
    )


def tile_attend_pagesandhidden_kernel(
    tc, pages_words, pages_scales, wa_words, wa_scales, notes_words, notes_scales, wb_words, wb_scales,
    kf, kf2, wo_words, wo_scales, wp_words, wp_scales, offs, offs2, out,
):
    nc = tc.nc
    with ExitStack() as ctx:
        keep = ctx.enter_context(tc.tile_pool(name="keep", bufs=1))
        psum = ctx.enter_context(tc.psum_pool(name="psum", bufs=8))

        def plane(name, width, engine=nc.vector):
            tile = keep.tile([P, width], U8, name=name, align_bytes=64)
            engine.memset(tile[:].bitcast(I32), 0)
            return tile

        def load_scale_rows(queue, tile, scales, quadrant):
            queue.dma_start(
                out=tile[:].bitcast(I32)[32 * quadrant : 32 * quadrant + 4, :],
                in_=scales[0].bitcast(I32)[4 * quadrant : 4 * quadrant + 4, :],
            )

        def load_fp8(queue, name, words, width):
            tile = keep.tile([P, width], I32, name=name, align_bytes=64)
            queue.dma_start(out=tile[:], in_=words[0].rearrange("p n t -> p (n t)").bitcast(I32))
            return tile

        def load_fp4(queue, name, words, width):
            tile = keep.tile([P, 2 * width], U8, name=name, align_bytes=64)
            queue.dma_start(out=tile[:].bitcast(I32), in_=words[0].bitcast(I32))
            return tile

        wb_s = plane("wb_s", K)
        notes_s = plane("notes_s", U)
        pages_s = plane("pages_s", T, nc.gpsimd)
        wa_s = plane("wa_s", K)
        wo_s = plane("wo_s", E)
        wp_s = plane("wp_s", E)

        wb_w = load_fp8(nc.sync, "wb_w", wb_words, K)
        notes_w = load_fp4(nc.scalar, "notes_w", notes_words, U)
        for q in range(4):
            load_scale_rows(nc.scalar if q else nc.sync, wb_s, wb_scales, q)
        load_scale_rows(nc.sync, notes_s, notes_scales, 0)
        pages_w = load_fp8(nc.sync, "pages_w", pages_words, T)
        for q in range(1, 4):
            load_scale_rows(nc.sync, notes_s, notes_scales, q)
        offsets = keep.tile([P, SLOTS // 16], U16, name="offsets")
        nc.sync.dma_start(offsets[:], offs)
        for q in range(4):
            load_scale_rows(nc.gpsimd if q < 2 else nc.sync, pages_s, pages_scales, q)
        wa_w = load_fp4(nc.sync, "wa_w", wa_words, K)
        kf_t = keep.tile([P, PACK], F32, name="kf_t")
        nc.sync.dma_start(out=kf_t[:], in_=kf.rearrange("(p t) o -> p (t o)", t=PACK))
        for q in range(4):
            load_scale_rows(nc.sync, wa_s, wa_scales, q)
        offsets2 = keep.tile([P, SLOTS // 16], U16, name="offsets2")
        nc.sync.dma_start(offsets2[:], offs2)
        kf2_t = keep.tile([P, PACK], F32, name="kf2_t")
        nc.sync.dma_start(out=kf2_t[:], in_=kf2.rearrange("(p t) o -> p (t o)", t=PACK))
        wo_w = load_fp4(nc.sync, "wo_w", wo_words, E)
        for q in range(4):
            load_scale_rows(nc.sync, wo_s, wo_scales, q)
        wp_w = load_fp8(nc.sync, "wp_w", wp_words, E)
        for q in range(4):
            load_scale_rows(nc.sync, wp_s, wp_scales, q)

        wb_wd = keep.tile([P, K], U32, name="wb_wd", align_bytes=64)
        deal(nc, wb_wd[:], wb_w[:].bitcast(U32), 4)
        wb_sd = keep.tile([P, K], U8, name="wb_sd", align_bytes=64)
        deal(nc, wb_sd[:], wb_s[:], 16)


        h1 = [keep.tile([P, U], F32, name="h1_%d" % t) for t in range(PACK)]
        for t in range(PACK):
            for b in range(U // BANK):
                acc = psum.tile([P, BANK], F32, name="acc")
                nc.tensor.matmul_mx(
                    out=acc[:],
                    lhsT=wb_wd[:, t * P : (t + 1) * P].bitcast(FP8X4),
                    lhsT_scale=wb_sd[:, t * P : (t + 1) * P],
                    rhs=notes_w[:, 2 * b * BANK : 2 * (b + 1) * BANK].bitcast(FP4X4),
                    rhs_scale=notes_s[:, b * BANK : (b + 1) * BANK],
                    start=True,
                    stop=True,
                )
                nc.scalar.copy(out=h1[t][:, b * BANK : (b + 1) * BANK], in_=acc[:])

        picked_w = [keep.tile([P, HALF], U32, name="picked_w%d" % h, align_bytes=64) for h in range(2)]
        picked_s = [keep.tile([P, HALF], U8, name="picked_s%d" % h, align_bytes=64) for h in range(2)]
        halves = [offsets[:, h * (HALF // 16) : (h + 1) * (HALF // 16)] for h in range(2)]
        nc.vector.tensor_copy(picked_w[0][:], pages_w[:].bitcast(U32).indirect(halves[0]))
        nc.vector.tensor_copy(picked_s[0][:], pages_s[:].indirect(halves[0]))
        nc.vector.tensor_copy(picked_w[1][:], pages_w[:].bitcast(U32).indirect(halves[1]))
        wa_wd = keep.tile([P, 2 * K], U8, name="wa_wd", align_bytes=64)
        deal(nc, wa_wd[:].bitcast(U16), wa_w[:].bitcast(U16), 8)
        wa_sd = keep.tile([P, K], U8, name="wa_sd", align_bytes=64)
        deal(nc, wa_sd[:], wa_s[:], 16)
        nc.vector.tensor_copy(picked_s[1][:], pages_s[:].indirect(halves[1]))

        w_bf = [keep.tile([P, HALF * PACK], BF16, name="w_bf%d" % h, align_bytes=64) for h in range(2)]
        w_q = keep.tile([P, SLOTS], U32, name="w_q", align_bytes=64)
        w_s = keep.tile([P, SLOTS], U8, name="w_s", align_bytes=64)
        for h in range(2):
            for c in range(HALF // CHUNK):
                cols = slice(c * CHUNK, (c + 1) * CHUNK)
                z = psum.tile([P, PACK, CHUNK], F32, name="acc")
                for t in range(PACK):
                    nc.tensor.matmul_mx(
                        out=z[:, t, :],
                        lhsT=wa_wd[:, 2 * t * P : 2 * (t + 1) * P].bitcast(FP4X4),
                        lhsT_scale=wa_sd[:, t * P : (t + 1) * P],
                        rhs=picked_w[h][:, cols].bitcast(FP8X4),
                        rhs_scale=picked_s[h][:, cols],
                        start=True,
                        stop=True,
                    )
                nc.vector.tensor_tensor(
                    out=w_bf[h][:, c * BANK : (c + 1) * BANK].rearrange("p (i t) -> p i t", t=PACK),
                    in0=z[:].rearrange("p t i -> p i t"),
                    in1=kf_t[:].unsqueeze(1).to_broadcast([P, CHUNK, PACK]),
                    op=MULT,
                )
        for h in range(2):
            cols = slice(h * HALF, (h + 1) * HALF)
            nc.vector.quantize_mx(out=w_q[:, cols].bitcast(FP8X4), scales=w_s[:, cols], in_=w_bf[h][:])

        first = 0
        for h, n in enumerate(STRETCHES):
            cols = slice(first, first + n)
            lists = offsets2[:, first // 16 : (first + n) // 16]
            first = first + n
            looked = keep.tile([P, PACK, n], F32, name="looked%d" % h)
            for t in range(PACK):
                if h == 1 and t < 2:
                    nc.vector.tensor_copy(looked[:, t, :], h1[t][:].indirect(lists))
                else:
                    nc.scalar.activation(looked[:, t, :], h1[t][:].indirect(lists), COPY)
            w2_bf = keep.tile([P, n * PACK], BF16, name="w2_bf%d" % h, align_bytes=64)
            nc.vector.tensor_tensor(
                out=w2_bf[:].rearrange("p (c i t) -> p c t i", t=PACK, i=4),
                in0=looked[:].rearrange("p t (c i) -> p c t i", i=4),
                in1=kf2_t[:].unsqueeze(1).unsqueeze(3).to_broadcast([P, n // 4, PACK, 4]),
                op=MULT,
            )
            w2_q = keep.tile([P, n], U32, name="w2_q%d" % h, align_bytes=64)
            w2_s = keep.tile([P, n], U8, name="w2_s%d" % h, align_bytes=64)
            nc.vector.quantize_mx(out=w2_q[:].bitcast(FP8X4), scales=w2_s[:], in_=w2_bf[:])
            acc = psum.tile([P, E // P, n], F32, name="acc")
            for a in range(E // P):
                nc.tensor.matmul_mx(
                    out=acc[:, a, :],
                    lhsT=wo_w[:, 2 * a * P : 2 * (a + 1) * P].bitcast(FP4X4),
                    lhsT_scale=wo_s[:, a * P : (a + 1) * P],
                    rhs=w_q[:, cols].bitcast(FP8X4),
                    rhs_scale=w_s[:, cols],
                    start=(a == 0),
                    stop=False,
                )
            for a in range(E // P):
                nc.tensor.matmul_mx(
                    out=acc[:, a, :],
                    lhsT=wp_w[:, a * P : (a + 1) * P].bitcast(FP8X4),
                    lhsT_scale=wp_s[:, a * P : (a + 1) * P],
                    rhs=w2_q[:].bitcast(FP8X4),
                    rhs_scale=w2_s[:],
                    start=False,
                    stop=(a == E // P - 1),
                )
            y = keep.tile([P, E // P, n], F32, name="y%d" % h)
            nc.scalar.copy(out=y[:], in_=acc[:])
            nc.sync.dma_start(out=out[:, cols].rearrange("(a p) i -> p a i", p=P), in_=y[:])
